import numpy as np
CORES = [2,42,66,74,82,90,114]
N = 7
TK = 256
D = 128 * N
EPS = 0.01
def setup_inputs(rng):
    x = rng.standard_normal((N, 128, TK), dtype=np.float32) * (0.5 + np.abs(rng.standard_normal((1, 1, TK), dtype=np.float32))) + rng.standard_normal((1, 1, TK), dtype=np.float32)
    return {"x": x, "dy": rng.standard_normal((N, 128, TK), dtype=np.float32) + 0.5 * x + rng.standard_normal((1, 1, TK), dtype=np.float32)}
def setup_inputs_big(rng):
    d = setup_inputs(rng)
    for k in ("x", "dy"): d[k] = (d[k].astype(np.float32) * 1024.0).astype(d[k].dtype)
    return d
def setup_inputs_small(rng):
    d = setup_inputs(rng)
    for k in ("x", "dy"): d[k] = (d[k].astype(np.float32) * (1 / 1024.0)).astype(d[k].dtype)
    return d
def setup_inputs_apart(rng):
    d = setup_inputs(rng)
    f = (10.0 ** rng.permutation(np.linspace(-1.5, 1.5, N))).astype(np.float32).reshape(N, 1, 1)
    for k in ("x",): d[k] = (d[k].astype(np.float32) * f).astype(d[k].dtype)
    return d
def setup_inputs_mixed(rng):
    d = setup_inputs(rng)
    f = (10.0 ** rng.uniform(-3, 3, (1, 1, TK))).astype(np.float32); shape = rng.integers(3, size=(1, 1, TK))
    for k in ("x", "dy"):
        x = d[k].astype(np.float32)
        m = x.mean(axis=(0, 1), keepdims=True); level = m + np.sign(x - m) * np.abs(x - m).mean(axis=(0, 1), keepdims=True) * rng.uniform(0.9, 1.1, x.shape).astype(np.float32)
        other = x * np.where(rng.random(x.shape) < 0.5, 0.1, 1.0).astype(np.float32)
        d[k] = (np.where(shape == 1, level, np.where(shape == 2, other, x)) * f).astype(d[k].dtype)
    return d
def setup_inputs_offset(rng):
    d = setup_inputs(rng)
    x = d["x"]; spread = x.std(axis=(0, 1), keepdims=True)
    d["x"] = (x + spread * rng.uniform(16, 48, (1, 1, TK)) * rng.choice([-1.0, 1.0], (1, 1, TK))).astype(np.float32)
    return d
def reference(x, dy):
    X, DY = x.astype(np.float64), dy.astype(np.float64)
    mu = X.sum(axis=(0, 1)) / D
    rs = 1.0 / np.sqrt(((X - mu) ** 2).sum(axis=(0, 1)) / D + EPS)
    n = (X - mu) * rs
    a = DY.sum(axis=(0, 1)) / D; c = (DY * n).sum(axis=(0, 1)) / D
    return {"dx": (rs * (DY - a - n * c)).astype(np.float32)}

@@ -1,0 +1,216 @@
+from concourse.bass import DstId, RemoteDMATransfer
+from concourse.mybir import AluOpType, AxisListType, ActivationFunctionType
+
+NR = 7
+D = 128 * NR
+EPS = 0.01
+BW = 8
+NEV = 48
+
+SCRATCH = {
+    "xF": ("sbuf", [128, 256], "float32"),
+    "dyF": ("sbuf", [128, 256], "float32"),
+    "ones": ("sbuf", [128, 128], "float32"),
+    "R": ("sbuf", [128, 131], "float32"),
+    "DI": ("sbuf", [128, 128], "float32"),
+    "st": ("sbuf", [128, 2, BW], "float32"),
+    "G": ("sbuf", [128, 16, BW], "float32"),
+    "rep": ("sbuf", [128, 14, 3], "float32"),
+    "T1": ("sbuf", [128, 8, BW], "float32"),
+    "T2": ("sbuf", [128, 4, BW], "float32"),
+    "S": ("sbuf", [128, 2, BW], "float32"),
+    "Ph": ("sbuf", [128, 2, 2], "float32"),
+    "Z": ("sbuf", [128, 2, 2], "float32"),
+    "W1": ("sbuf", [128, 2, 2], "float32"),
+    "W2": ("sbuf", [128, 2, 2], "float32"),
+    "sd": ("sbuf", [128, 2], "float32"),
+    "w": ("sbuf", [128, 2], "float32"),
+    "k": ("sbuf", [128, 2], "float32"),
+    "tk": ("sbuf", [128, 2], "float32"),
+    "ao": ("sbuf", [128, 2], "float32"),
+    "am": ("sbuf", [128, 2], "float32"),
+    "a2": ("sbuf", [128, 2], "float32"),
+    "C": ("sbuf", [128, 2], "float32"),
+    "xc": ("sbuf", [128, 256], "float32"),
+    "junk": ("sbuf", [128, 256], "float32"),
+    "prod": ("sbuf", [128, 256], "float32"),
+    "u": ("sbuf", [128, 256], "float32"),
+    "v": ("sbuf", [128, 256], "float32"),
+    "diag": ("sbuf", [128, 256], "float32"),
+    "outb": ("sbuf", [128, 256], "float32"),
+    "psx0": ("psum", [128, 512], "float32"),
+    "psx1": ("psum", [128, 512], "float32"),
+    "psd0": ("psum", [128, 512], "float32"),
+    "psd1": ("psum", [128, 512], "float32"),
+    "pso0": ("psum", [128, 512], "float32"),
+    "pso1": ("psum", [128, 512], "float32"),
+}
+SEMAPHORES = ["ldx", "ldy", "ms", "stat", "repd", "arr", "loc", "st0", "st1"] + ["e%d" % i for i in range(NEV)]
+
+
+def _send_mask(topo, src, dsts):
+    m = None
+    for d in dsts:
+        if not topo.may_write(src, d):
+            raise ValueError("core %d may not write to core %d" % (src, d))
+        m = topo.mask(src, d) if m is None else (m & topo.mask(src, d))
+    return m, bin(m).count("1")
+
+
+def rank_program(g, core, T, topo):
+    rank = T.rank_of(core)
+    if rank is None:
+        return
+    V, A, P, Q = g.vector, g.scalar, g.tensor, g.sync
+    add, sub, mul = AluOpType.add, AluOpType.subtract, AluOpType.mult
+    F = ActivationFunctionType
+    sem = T.sem
+    cnt = [0]
+
+    def ev():
+        cnt[0] += 1
+        return sem["e%d" % (cnt[0] - 1)]
+
+    H = [slice(0, 128), slice(128, 256)]
+    psx, psd, pso = [T.psx0, T.psx1], [T.psd0, T.psd1], [T.pso0, T.pso1]
+
+    Q.dma_start(T.xF[:], T.x[:]).then_inc(sem.ldx, 16)
+    A.dma_start(T.dyF[:], T.dy[:]).then_inc(sem.ldy, 16)
+
+    fills = [
+        (T.ones[:], 1.0),
+        (T.R[:, 0:1], -1.0), (T.R[:, 129:130], -1.0 / 128.0), (T.R[:, 130:131], -1.0),
+        (T.G[:, 14:16, 0:4], 0.0), (T.G[:, 14:16, 4:5], D * EPS), (T.G[:, 14:16, 5:BW], 0.0),
+        (T.st[:, :, 5:BW], 0.0),
+    ]
+    for ap, c in fills:
+        V.memset(ap, c).then_inc(sem.ms, 1)
+    M = len(fills)
+    e_id, e_di = ev(), ev()
+    g.wait_ge(sem.ms, M)
+    g.affine_select(T.R[:, 1:129], T.ones[:], [[-1, 128]], AluOpType.is_equal, 0.0, 0, 1).then_inc(e_id, 1)
+    V.wait_ge(sem.ms, M)
+    V.wait_ge(e_id, 1)
+    V.tensor_scalar(T.DI[:], T.R[:, 1:129], float(D), None, mul).then_inc(e_di, 1)
+
+    e_px, e_pd = [ev(), ev()], [ev(), ev()]
+    P.wait_ge(sem.ms, M)
+    P.wait_ge(e_id, 1)
+    P.wait_ge(sem.ldx, 16)
+    for h in range(2):
+        P.matmul(psx[h][:, 0:130], T.xF[:, H[h]], T.R[:, 1:131], True, True).then_inc(e_px[h], 1)
+    P.wait_ge(sem.ldy, 16)
+    for h in range(2):
+        P.matmul(psd[h][:, 0:129], T.dyF[:, H[h]], T.R[:, 0:129], True, True).then_inc(e_pd[h], 1)
+
+    e_xc, e_pr = [ev(), ev()], [ev(), ev()]
+    for h in range(2):
+        V.wait_ge(e_px[h], 1)
+        V.tensor_scalar(T.xc[:, H[h]], psx[h][:, 0:128], psx[h][:, 128:129], None, add).then_inc(e_xc[h], 1)
+        V.tensor_copy(T.st[:, h, 1:3], psx[h][:, 128:130]).then_inc(sem.stat, 1)
+        A.wait_ge(e_xc[h], 1)
+        A.activation(T.junk[:, H[h]], T.xc[:, H[h]], F.Square, accum_out=T.st[:, h, 4:5]).then_inc(sem.stat, 1)
+    for h in range(2):
+        V.wait_ge(e_pd[h], 1)
+        V.wait_ge(e_xc[h], 1)
+        V.tensor_tensor(T.prod[:, H[h]], psd[h][:, 1:129], T.xc[:, H[h]], mul).then_inc(e_pr[h], 1)
+        if h == 0:
+            V.tensor_copy(T.st[:, h, 0:1], psd[h][:, 0:1]).then_inc(sem.stat, 1)
+        else:
+            A.wait_ge(e_pr[h], 1)
+            A.activation(T.st[:, h, 0:1], psd[h][:, 0:1], F.Copy).then_inc(sem.stat, 1)
+        V.wait_ge(e_pr[h], 1)
+        V.tensor_reduce(T.st[:, h, 3:4], T.prod[:, H[h]], AxisListType.X, add).then_inc(sem.stat, 1)
+    NSTAT = 8
+
+    others = [c for c in T.cores if c != core]
+    mask, _ = _send_mask(topo, core, others)
+    ids = []
+    for c in others:
+        rid, pid, _se = topo.addr(c)
+        ids.append(DstId(rid=rid, pnc=pid))
+    slot = T.G[:, 2 * rank:2 * rank + 2, :]
+    g.wait_ge(sem.stat, NSTAT)
+    g.remote_dma_fused([RemoteDMATransfer(dst_ids=ids, dma_engine_mask=mask, remote_sem=sem.arr,
+                                          srcs=[T.st[:]], dsts=[slot for _ in others], alu_op=0)],
+                       local_sem=sem.loc)
+    expected = 0
+    for s in others:
+        expected += _send_mask(topo, s, [c for c in T.cores if c != s])[1]
+
+    e_own, e_ao = ev(), ev()
+    V.wait_ge(sem.stat, NSTAT)
+    V.tensor_copy(slot, T.st[:]).then_inc(e_own, 1)
+    for r in range(NR):
+        V.tensor_copy(T.rep[:, 2 * r:2 * r + 2, :], T.st[:, :, 0:3]).then_inc(sem.repd, 1)
+    V.tensor_scalar(T.ao[:], T.st[:, :, 0], -1.0 / 128.0, None, mul).then_inc(e_ao, 1)
+
+    V.wait_ge(e_own, 1)
+    V.wait_ge(sem.repd, NR)
+    V.wait_ge(sem.arr, expected)
+    e = [ev() for _ in range(9)]
+    V.tensor_tensor(T.G[:, 0:14, 0:3], T.G[:, 0:14, 0:3], T.rep[:], sub).then_inc(e[0], 1)
+    V.wait_ge(e[0], 1)
+    V.tensor_tensor(T.G[:, 0:14, 5:7], T.G[:, 0:14, 1:3], T.G[:, 0:14, 0:2], mul).then_inc(e[1], 1)
+    V.wait_ge(e[1], 1)
+    V.tensor_tensor(T.T1[:], T.G[:, 0:8, :], T.G[:, 8:16, :], add).then_inc(e[2], 1)
+    V.wait_ge(e[2], 1)
+    V.tensor_tensor(T.T2[:], T.T1[:, 0:4, :], T.T1[:, 4:8, :], add).then_inc(e[3], 1)
+    V.wait_ge(e[3], 1)
+    V.tensor_tensor(T.S[:], T.T2[:, 0:2, :], T.T2[:, 2:4, :], add).then_inc(e[4], 1)
+    V.wait_ge(e[4], 1)
+    V.tensor_scalar(T.Ph[:], T.S[:, :, 1:3], -1.0 / NR, None, mul).then_inc(e[5], 1)
+    V.tensor_tensor(T.W1[:], T.S[:, :, 3:5], T.S[:, :, 5:7], add).then_inc(e[6], 1)
+    V.wait_ge(e[5], 1)
+    V.tensor_tensor(T.Z[:], T.Ph[:], T.S[:, :, 0:2], mul).then_inc(e[7], 1)
+    V.wait_ge(e[6], 1)
+    V.wait_ge(e[7], 1)
+    V.tensor_tensor(T.W2[:], T.W1[:], T.Z[:], add).then_inc(e[8], 1)
+
+    e_sd = ev()
+    A.wait_ge(e[8], 1)
+    A.activation(T.sd[:], T.W2[:, :, 1], F.Sqrt, scale=1.0 / D).then_inc(e_sd, 1)
+
+    e_w, e_k, e_t, e_a, e_a2, e_c = ev(), ev(), ev(), ev(), ev(), ev()
+    V.wait_ge(e[8], 1)
+    V.reciprocal(T.w[:], T.W2[:, :, 1]).then_inc(e_w, 1)
+    V.tensor_scalar(T.am[:], T.S[:, :, 0], -1.0 / D, None, mul).then_inc(e_a, 1)
+    V.wait_ge(e_w, 1)
+    V.tensor_tensor(T.k[:], T.W2[:, :, 0], T.w[:], mul).then_inc(e_k, 1)
+    V.wait_ge(e_a, 1)
+    V.wait_ge(e_ao, 1)
+    V.tensor_tensor(T.a2[:], T.am[:], T.ao[:], add).then_inc(e_a2, 1)
+    V.wait_ge(e_k, 1)
+    V.tensor_tensor(T.tk[:], T.Ph[:, :, 0], T.k[:], mul).then_inc(e_t, 1)
+    V.wait_ge(e_t, 1)
+    V.wait_ge(e_a2, 1)
+    V.tensor_tensor(T.C[:], T.a2[:], T.tk[:], sub).then_inc(e_c, 1)
+    V.wait_ge(e_c, 1)
+    e_u, e_v, e_dg, e_o = [ev(), ev()], [ev(), ev()], [ev(), ev()], [ev(), ev()]
+    for h in range(2):
+        V.tensor_scalar(T.u[:, H[h]], T.xc[:, H[h]], T.k[:, h:h + 1], T.C[:, h:h + 1], mul, add).then_inc(e_u[h], 1)
+    for h in range(2):
+        V.wait_ge(e_u[h], 1)
+        V.tensor_tensor(T.v[:, H[h]], psd[h][:, 1:129], T.u[:, H[h]], sub).then_inc(e_v[h], 1)
+    V.wait_ge(e_di, 1)
+    V.wait_ge(e_sd, 1)
+    for h in range(2):
+        V.tensor_scalar(T.diag[:, H[h]], T.DI[:], T.sd[:, h:h + 1], T.w[:, h:h + 1], mul, mul).then_inc(e_dg[h], 1)
+
+    for h in range(2):
+        P.wait_ge(e_v[h], 1)
+        P.wait_ge(e_dg[h], 1)
+        P.matmul(pso[h][:, 0:128], T.v[:, H[h]], T.diag[:, H[h]], True, True).then_inc(e_o[h], 1)
+    e_c0, e_c1 = ev(), ev()
+    A.wait_ge(e_o[0], 1)
+    A.activation(T.outb[:, H[0]], pso[0][:, 0:128], F.Copy).then_inc(e_c0, 1)
+    A.wait_ge(e_c0, 1)
+    A.dma_start(T.dx[:, H[0]], T.outb[:, H[0]]).then_inc(sem.st0, 16)
+    V.wait_ge(e_o[1], 1)
+    V.tensor_copy(T.outb[:, H[1]], pso[1][:, 0:128]).then_inc(e_c1, 1)
+    Q.wait_ge(e_c1, 1)
+    Q.dma_start(T.dx[:, H[1]], T.outb[:, H[1]]).then_inc(sem.st1, 16)
+
+    g.wait_ge(sem.loc, bin(mask).count("1"))
+    A.wait_ge(sem.st0, 16)
+    Q.wait_ge(sem.st1, 16)

@@ -4,8 +4,10 @@ from concourse.mybir import AluOpType, AxisListType, ActivationFunctionType
 NR = 7
 D = 128 * NR
 EPS = 0.01
-BW = 8
-NEV = 48
+SW = 16
+NEV = 64
+NCH = 4
+CW = 256 // NCH
 
 SCRATCH = {
     "xF": ("sbuf", [128, 256], "float32"),
@@ -13,39 +15,39 @@ SCRATCH = {
     "ones": ("sbuf", [128, 128], "float32"),
     "R": ("sbuf", [128, 131], "float32"),
     "DI": ("sbuf", [128, 128], "float32"),
-    "st": ("sbuf", [128, 2, BW], "float32"),
-    "G": ("sbuf", [128, 16, BW], "float32"),
-    "rep": ("sbuf", [128, 14, 3], "float32"),
-    "T1": ("sbuf", [128, 8, BW], "float32"),
-    "T2": ("sbuf", [128, 4, BW], "float32"),
-    "S": ("sbuf", [128, 2, BW], "float32"),
-    "Ph": ("sbuf", [128, 2, 2], "float32"),
-    "Z": ("sbuf", [128, 2, 2], "float32"),
-    "W1": ("sbuf", [128, 2, 2], "float32"),
-    "W2": ("sbuf", [128, 2, 2], "float32"),
-    "sd": ("sbuf", [128, 2], "float32"),
+    "st": ("sbuf", [128, SW], "float32"),
+    "G": ("sbuf", [128, 8, SW], "float32"),
+    "rep": ("sbuf", [128, 7, 6], "float32"),
+    "T1": ("sbuf", [128, 4, SW], "float32"),
+    "T2": ("sbuf", [128, 2, SW], "float32"),
+    "S": ("sbuf", [128, SW], "float32"),
+    "Ph": ("sbuf", [128, 4], "float32"),
+    "Z": ("sbuf", [128, 4], "float32"),
+    "W1": ("sbuf", [128, 4], "float32"),
+    "W2": ("sbuf", [128, 4], "float32"),
     "w": ("sbuf", [128, 2], "float32"),
     "k": ("sbuf", [128, 2], "float32"),
-    "tk": ("sbuf", [128, 2], "float32"),
-    "ao": ("sbuf", [128, 2], "float32"),
-    "am": ("sbuf", [128, 2], "float32"),
-    "a2": ("sbuf", [128, 2], "float32"),
-    "C": ("sbuf", [128, 2], "float32"),
+    "aon": ("sbuf", [128, 2], "float32"),
+    "nega": ("sbuf", [128, 2], "float32"),
     "xc": ("sbuf", [128, 256], "float32"),
     "junk": ("sbuf", [128, 256], "float32"),
     "prod": ("sbuf", [128, 256], "float32"),
     "u": ("sbuf", [128, 256], "float32"),
     "v": ("sbuf", [128, 256], "float32"),
-    "diag": ("sbuf", [128, 256], "float32"),
+    "dz": ("sbuf", [128, 256], "float32"),
+    "dw": ("sbuf", [128, 256], "float32"),
+    "sdB": ("sbuf", [128, 256], "float32"),
     "outb": ("sbuf", [128, 256], "float32"),
     "psx0": ("psum", [128, 512], "float32"),
     "psx1": ("psum", [128, 512], "float32"),
     "psd0": ("psum", [128, 512], "float32"),
     "psd1": ("psum", [128, 512], "float32"),
-    "pso0": ("psum", [128, 512], "float32"),
-    "pso1": ("psum", [128, 512], "float32"),
+    "y0": ("psum", [128, 512], "float32"),
+    "y1": ("psum", [128, 512], "float32"),
+    "y2": ("psum", [128, 512], "float32"),
 }
-SEMAPHORES = ["ldx", "ldy", "ms", "stat", "repd", "arr", "loc", "st0", "st1"] + ["e%d" % i for i in range(NEV)]
+SEMAPHORES = (["ldx", "ldy", "ms", "first", "stat", "repd", "arr", "loc", "st0", "st1", "cp0", "cp1"]
+              + ["e%d" % i for i in range(NEV)])
 
 
 def _send_mask(topo, src, dsts):
@@ -55,6 +57,11 @@ def _send_mask(topo, src, dsts):
             raise ValueError("core %d may not write to core %d" % (src, d))
         m = topo.mask(src, d) if m is None else (m & topo.mask(src, d))
     return m, bin(m).count("1")
+
+
+def _plan(cores, r):
+    nxt = cores[(r + 1) % len(cores)]
+    return nxt, [c for c in cores if c != cores[r] and c != nxt]
 
 
 def rank_program(g, core, T, topo):
@@ -72,16 +79,16 @@ def rank_program(g, core, T, topo):
         return sem["e%d" % (cnt[0] - 1)]
 
     H = [slice(0, 128), slice(128, 256)]
-    psx, psd, pso = [T.psx0, T.psx1], [T.psd0, T.psd1], [T.pso0, T.pso1]
+    psx, psd = [T.psx0, T.psx1], [T.psd0, T.psd1]
 
     Q.dma_start(T.xF[:], T.x[:]).then_inc(sem.ldx, 16)
     A.dma_start(T.dyF[:], T.dy[:]).then_inc(sem.ldy, 16)
 
     fills = [
         (T.ones[:], 1.0),
-        (T.R[:, 0:1], -1.0), (T.R[:, 129:130], -1.0 / 128.0), (T.R[:, 130:131], -1.0),
-        (T.G[:, 14:16, 0:4], 0.0), (T.G[:, 14:16, 4:5], D * EPS), (T.G[:, 14:16, 5:BW], 0.0),
-        (T.st[:, :, 5:BW], 0.0),
+        (T.R[:, 0:1], -1.0), (T.R[:, 129:130], -1.0), (T.R[:, 130:131], -1.0 / 128.0),
+        (T.G[:, 7, 0:6], 0.0), (T.G[:, 7, 6:8], D * EPS), (T.G[:, 7, 8:SW], 0.0),
+        (T.st[:, 10:SW], 0.0),
     ]
     for ap, c in fills:
         V.memset(ap, c).then_inc(sem.ms, 1)
@@ -94,123 +101,155 @@ def rank_program(g, core, T, topo):
     V.tensor_scalar(T.DI[:], T.R[:, 1:129], float(D), None, mul).then_inc(e_di, 1)
 
     e_px, e_pd = [ev(), ev()], [ev(), ev()]
+    e_xc, e_pr = [ev(), ev()], [ev(), ev()]
     P.wait_ge(sem.ms, M)
     P.wait_ge(e_id, 1)
     P.wait_ge(sem.ldx, 16)
     for h in range(2):
         P.matmul(psx[h][:, 0:130], T.xF[:, H[h]], T.R[:, 1:131], True, True).then_inc(e_px[h], 1)
+        V.wait_ge(e_px[h], 1)
+        V.tensor_copy(T.st[:, h:h + 3:2], psx[h][:, 128:130]).then_inc(sem.first, 1)
+        V.tensor_scalar(T.xc[:, H[h]], psx[h][:, 0:128], psx[h][:, 129:130], None, add).then_inc(e_xc[h], 1)
+        A.wait_ge(e_xc[h], 1)
+        A.activation(T.junk[:, H[h]], T.xc[:, H[h]], F.Square, accum_out=T.st[:, 6 + h:7 + h]).then_inc(sem.stat, 1)
     P.wait_ge(sem.ldy, 16)
     for h in range(2):
         P.matmul(psd[h][:, 0:129], T.dyF[:, H[h]], T.R[:, 0:129], True, True).then_inc(e_pd[h], 1)
-
-    e_xc, e_pr = [ev(), ev()], [ev(), ev()]
-    for h in range(2):
-        V.wait_ge(e_px[h], 1)
-        V.tensor_scalar(T.xc[:, H[h]], psx[h][:, 0:128], psx[h][:, 128:129], None, add).then_inc(e_xc[h], 1)
-        V.tensor_copy(T.st[:, h, 1:3], psx[h][:, 128:130]).then_inc(sem.stat, 1)
-        A.wait_ge(e_xc[h], 1)
-        A.activation(T.junk[:, H[h]], T.xc[:, H[h]], F.Square, accum_out=T.st[:, h, 4:5]).then_inc(sem.stat, 1)
-    for h in range(2):
         V.wait_ge(e_pd[h], 1)
         V.wait_ge(e_xc[h], 1)
         V.tensor_tensor(T.prod[:, H[h]], psd[h][:, 1:129], T.xc[:, H[h]], mul).then_inc(e_pr[h], 1)
         if h == 0:
-            V.tensor_copy(T.st[:, h, 0:1], psd[h][:, 0:1]).then_inc(sem.stat, 1)
+            V.tensor_copy(T.st[:, 4:5], psd[h][:, 0:1]).then_inc(sem.stat, 1)
         else:
             A.wait_ge(e_pr[h], 1)
-            A.activation(T.st[:, h, 0:1], psd[h][:, 0:1], F.Copy).then_inc(sem.stat, 1)
+            A.activation(T.st[:, 5:6], psd[h][:, 0:1], F.Copy).then_inc(sem.stat, 1)
         V.wait_ge(e_pr[h], 1)
-        V.tensor_reduce(T.st[:, h, 3:4], T.prod[:, H[h]], AxisListType.X, add).then_inc(sem.stat, 1)
-    NSTAT = 8
+        V.tensor_reduce(T.st[:, 8 + h:9 + h], T.prod[:, H[h]], AxisListType.X, add).then_inc(sem.stat, 1)
+    NSTAT = 6
 
-    others = [c for c in T.cores if c != core]
-    mask, _ = _send_mask(topo, core, others)
+    nxt, rest = _plan(T.cores, rank)
+    m1, b1 = _send_mask(topo, core, [nxt])
+    m5, b5 = _send_mask(topo, core, rest)
+    rid1, pid1, _se1 = topo.addr(nxt)
     ids = []
-    for c in others:
+    for c in rest:
         rid, pid, _se = topo.addr(c)
         ids.append(DstId(rid=rid, pnc=pid))
-    slot = T.G[:, 2 * rank:2 * rank + 2, :]
+    g.wait_ge(sem.first, 2)
+    g.remote_dma(T.G[:, rank, 0:4], T.st[:, 0:4], sem.arr, sem.loc, pid1, rid1, m1)
     g.wait_ge(sem.stat, NSTAT)
-    g.remote_dma_fused([RemoteDMATransfer(dst_ids=ids, dma_engine_mask=mask, remote_sem=sem.arr,
-                                          srcs=[T.st[:]], dsts=[slot for _ in others], alu_op=0)],
+    g.remote_dma_fused([RemoteDMATransfer(dst_ids=ids, dma_engine_mask=m5, remote_sem=sem.arr,
+                                          srcs=[T.st[:]], dsts=[T.G[:, rank, :] for _ in rest], alu_op=0)],
                        local_sem=sem.loc)
+    g.remote_dma(T.G[:, rank, 4:SW], T.st[:, 4:SW], sem.arr, sem.loc, pid1, rid1, m1)
     expected = 0
-    for s in others:
-        expected += _send_mask(topo, s, [c for c in T.cores if c != s])[1]
-
-    e_own, e_ao = ev(), ev()
-    V.wait_ge(sem.stat, NSTAT)
-    V.tensor_copy(slot, T.st[:]).then_inc(e_own, 1)
     for r in range(NR):
-        V.tensor_copy(T.rep[:, 2 * r:2 * r + 2, :], T.st[:, :, 0:3]).then_inc(sem.repd, 1)
-    V.tensor_scalar(T.ao[:], T.st[:, :, 0], -1.0 / 128.0, None, mul).then_inc(e_ao, 1)
+        if r != rank:
+            n_r, rest_r = _plan(T.cores, r)
+            if n_r == core:
+                expected += 2 * _send_mask(topo, T.cores[r], [core])[1]
+            else:
+                expected += _send_mask(topo, T.cores[r], rest_r)[1]
+
+    e_own, e_aon = ev(), ev()
+    V.wait_ge(sem.first, 2)
+    V.wait_ge(sem.stat, NSTAT)
+    V.tensor_copy(T.G[:, rank, :], T.st[:]).then_inc(e_own, 1)
+    for r in range(NR):
+        V.tensor_copy(T.rep[:, r, :], T.st[:, 0:6]).then_inc(sem.repd, 1)
+    V.tensor_scalar(T.aon[:], T.st[:, 4:6], 1.0 / 128.0, None, mul).then_inc(e_aon, 1)
 
     V.wait_ge(e_own, 1)
     V.wait_ge(sem.repd, NR)
     V.wait_ge(sem.arr, expected)
     e = [ev() for _ in range(9)]
-    V.tensor_tensor(T.G[:, 0:14, 0:3], T.G[:, 0:14, 0:3], T.rep[:], sub).then_inc(e[0], 1)
+    V.tensor_tensor(T.G[:, 0:7, 0:6], T.G[:, 0:7, 0:6], T.rep[:], sub).then_inc(e[0], 1)
     V.wait_ge(e[0], 1)
-    V.tensor_tensor(T.G[:, 0:14, 5:7], T.G[:, 0:14, 1:3], T.G[:, 0:14, 0:2], mul).then_inc(e[1], 1)
+    V.tensor_tensor(T.G[:, 0:7, 10:14], T.G[:, 0:7, 0:4], T.G[:, 0:7, 2:6], mul).then_inc(e[1], 1)
     V.wait_ge(e[1], 1)
-    V.tensor_tensor(T.T1[:], T.G[:, 0:8, :], T.G[:, 8:16, :], add).then_inc(e[2], 1)
+    V.tensor_tensor(T.T1[:], T.G[:, 0:4, :], T.G[:, 4:8, :], add).then_inc(e[2], 1)
     V.wait_ge(e[2], 1)
-    V.tensor_tensor(T.T2[:], T.T1[:, 0:4, :], T.T1[:, 4:8, :], add).then_inc(e[3], 1)
+    V.tensor_tensor(T.T2[:], T.T1[:, 0:2, :], T.T1[:, 2:4, :], add).then_inc(e[3], 1)
     V.wait_ge(e[3], 1)
-    V.tensor_tensor(T.S[:], T.T2[:, 0:2, :], T.T2[:, 2:4, :], add).then_inc(e[4], 1)
+    V.tensor_tensor(T.S[:], T.T2[:, 0, :], T.T2[:, 1, :], add).then_inc(e[4], 1)
     V.wait_ge(e[4], 1)
-    V.tensor_scalar(T.Ph[:], T.S[:, :, 1:3], -1.0 / NR, None, mul).then_inc(e[5], 1)
-    V.tensor_tensor(T.W1[:], T.S[:, :, 3:5], T.S[:, :, 5:7], add).then_inc(e[6], 1)
+    V.tensor_scalar(T.Ph[:], T.S[:, 0:4], -1.0 / NR, None, mul).then_inc(e[5], 1)
+    V.tensor_tensor(T.W1[:], T.S[:, 6:10], T.S[:, 10:14], add).then_inc(e[6], 1)
     V.wait_ge(e[5], 1)
-    V.tensor_tensor(T.Z[:], T.Ph[:], T.S[:, :, 0:2], mul).then_inc(e[7], 1)
+    V.tensor_tensor(T.Z[:], T.Ph[:], T.S[:, 2:6], mul).then_inc(e[7], 1)
     V.wait_ge(e[6], 1)
     V.wait_ge(e[7], 1)
     V.tensor_tensor(T.W2[:], T.W1[:], T.Z[:], add).then_inc(e[8], 1)
 
-    e_sd = ev()
-    A.wait_ge(e[8], 1)
-    A.activation(T.sd[:], T.W2[:, :, 1], F.Sqrt, scale=1.0 / D).then_inc(e_sd, 1)
+    e_ng, e_dya = [ev(), ev()], [ev(), ev()]
+    A.wait_ge(e[4], 1)
+    A.wait_ge(e_aon, 1)
+    A.wait_ge(sem.stat, NSTAT)
+    A.wait_ge(e_pr[0], 1)
+    for h in range(2):
+        A.activation(T.nega[:, h:h + 1], T.S[:, 4 + h:5 + h], F.Identity, bias=T.aon[:, h:h + 1],
+                     scale=1.0 / D).then_inc(e_ng[h], 1)
+    for h in range(2):
+        A.wait_ge(e_ng[h], 1)
+        A.activation(psd[h][:, 1:129], psd[h][:, 1:129], F.Identity, bias=T.nega[:, h:h + 1]).then_inc(e_dya[h], 1)
 
-    e_w, e_k, e_t, e_a, e_a2, e_c = ev(), ev(), ev(), ev(), ev(), ev()
+    half = [(c * CW) // 128 for c in range(NCH)]
+    low = [c * CW - 128 * half[c] for c in range(NCH)]
+    col = [slice(c * CW, (c + 1) * CW) for c in range(NCH)]
+    bc = [T.psx0[:, 0:CW]] + [T.psx1[:, (c - 1) * CW:c * CW] for c in range(1, NCH)]
+    yt = [T.y0[:, 0:CW], T.y0[:, CW:2 * CW], T.y1[:, 0:CW], T.y2[:, 0:CW]]
+    e_dz, e_bc, e_dw, e_vt, e_s = ([ev() for _ in range(NCH)] for _ in range(5))
+
     V.wait_ge(e[8], 1)
-    V.reciprocal(T.w[:], T.W2[:, :, 1]).then_inc(e_w, 1)
-    V.tensor_scalar(T.am[:], T.S[:, :, 0], -1.0 / D, None, mul).then_inc(e_a, 1)
+    for c in range(NCH):
+        h = half[c]
+        V.tensor_scalar(T.dz[:, col[c]], T.R[:, 1 + low[c]:1 + low[c] + CW], T.W2[:, h:h + 1], None,
+                        mul).then_inc(e_dz[c], 1)
+    e_w, e_k = ev(), ev()
+    e_u, e_v = [ev(), ev()], [ev(), ev()]
+    V.reciprocal(T.w[:], T.W2[:, 0:2]).then_inc(e_w, 1)
     V.wait_ge(e_w, 1)
-    V.tensor_tensor(T.k[:], T.W2[:, :, 0], T.w[:], mul).then_inc(e_k, 1)
-    V.wait_ge(e_a, 1)
-    V.wait_ge(e_ao, 1)
-    V.tensor_tensor(T.a2[:], T.am[:], T.ao[:], add).then_inc(e_a2, 1)
+    V.tensor_tensor(T.k[:], T.W2[:, 2:4], T.w[:], mul).then_inc(e_k, 1)
     V.wait_ge(e_k, 1)
-    V.tensor_tensor(T.tk[:], T.Ph[:, :, 0], T.k[:], mul).then_inc(e_t, 1)
-    V.wait_ge(e_t, 1)
-    V.wait_ge(e_a2, 1)
-    V.tensor_tensor(T.C[:], T.a2[:], T.tk[:], sub).then_inc(e_c, 1)
-    V.wait_ge(e_c, 1)
-    e_u, e_v, e_dg, e_o = [ev(), ev()], [ev(), ev()], [ev(), ev()], [ev(), ev()]
-    for h in range(2):
-        V.tensor_scalar(T.u[:, H[h]], T.xc[:, H[h]], T.k[:, h:h + 1], T.C[:, h:h + 1], mul, add).then_inc(e_u[h], 1)
-    for h in range(2):
-        V.wait_ge(e_u[h], 1)
-        V.tensor_tensor(T.v[:, H[h]], psd[h][:, 1:129], T.u[:, H[h]], sub).then_inc(e_v[h], 1)
     V.wait_ge(e_di, 1)
-    V.wait_ge(e_sd, 1)
     for h in range(2):
-        V.tensor_scalar(T.diag[:, H[h]], T.DI[:], T.sd[:, h:h + 1], T.w[:, h:h + 1], mul, mul).then_inc(e_dg[h], 1)
+        V.tensor_scalar(T.u[:, H[h]], T.xc[:, H[h]], T.Ph[:, 2 + h:3 + h], T.k[:, h:h + 1], sub, mul).then_inc(e_u[h], 1)
+        V.wait_ge(e_u[h], 1)
+        V.wait_ge(e_dya[h], 1)
+        V.tensor_tensor(T.v[:, H[h]], psd[h][:, 1:129], T.u[:, H[h]], sub).then_inc(e_v[h], 1)
+        for c in range(NCH):
+            if half[c] == h:
+                V.tensor_scalar(T.dw[:, col[c]], T.DI[:, low[c]:low[c] + CW], T.w[:, h:h + 1], None,
+                                mul).then_inc(e_dw[c], 1)
 
-    for h in range(2):
-        P.wait_ge(e_v[h], 1)
-        P.wait_ge(e_dg[h], 1)
-        P.matmul(pso[h][:, 0:128], T.v[:, H[h]], T.diag[:, H[h]], True, True).then_inc(e_o[h], 1)
-    e_c0, e_c1 = ev(), ev()
-    A.wait_ge(e_o[0], 1)
-    A.activation(T.outb[:, H[0]], pso[0][:, 0:128], F.Copy).then_inc(e_c0, 1)
-    A.wait_ge(e_c0, 1)
-    A.dma_start(T.dx[:, H[0]], T.outb[:, H[0]]).then_inc(sem.st0, 16)
-    V.wait_ge(e_o[1], 1)
-    V.tensor_copy(T.outb[:, H[1]], pso[1][:, 0:128]).then_inc(e_c1, 1)
-    Q.wait_ge(e_c1, 1)
-    Q.dma_start(T.dx[:, H[1]], T.outb[:, H[1]]).then_inc(sem.st1, 16)
+    for c in range(NCH):
+        P.wait_ge(e_dz[c], 1)
+        P.matmul(bc[c], T.ones[:], T.dz[:, col[c]], True, True).then_inc(e_bc[c], 1)
+    for c in range(NCH):
+        P.wait_ge(e_v[half[c]], 1)
+        P.wait_ge(e_dw[c], 1)
+        P.matmul(yt[c], T.v[:, H[half[c]]], T.dw[:, col[c]], True, True).then_inc(e_vt[c], 1)
 
-    g.wait_ge(sem.loc, bin(mask).count("1"))
-    A.wait_ge(sem.st0, 16)
-    Q.wait_ge(sem.st1, 16)
+    for c in range(NCH):
+        if c == 0:
+            A.wait_ge(e_bc[0], 1)
+        elif c == 1:
+            for j in range(1, NCH):
+                A.wait_ge(e_bc[j], 1)
+        A.activation(T.sdB[:, col[c]], bc[c], F.Sqrt, scale=1.0 / D).then_inc(e_s[c], 1)
+
+    cp = [sem.cp0, sem.cp1]
+    V.wait_ge(e_vt[0], 1)
+    V.wait_ge(e_vt[1], 1)
+    for c in range(NCH):
+        V.wait_ge(e_vt[c], 1)
+        V.wait_ge(e_s[c], 1)
+        V.tensor_tensor(T.outb[:, col[c]], yt[c], T.sdB[:, col[c]], mul).then_inc(cp[half[c]], 1)
+    Q.wait_ge(cp[0], NCH // 2)
+    Q.dma_start(T.dx[:, H[0]], T.outb[:, H[0]]).then_inc(sem.st0, 16)
+    A.wait_ge(cp[1], NCH // 2)
+    A.dma_start(T.dx[:, H[1]], T.outb[:, H[1]]).then_inc(sem.st1, 16)
+
+    g.wait_ge(sem.loc, 2 * b1 + b5)
+    Q.wait_ge(sem.st0, 16)
+    A.wait_ge(sem.st1, 16)

@@ -14,7 +14,9 @@ SCRATCH = {
     "dyF": ("sbuf", [128, 256], "float32"),
     "ones": ("sbuf", [128, 128], "float32"),
     "R": ("sbuf", [128, 131], "float32"),
-    "DI": ("sbuf", [128, 128], "float32"),
+    "Dc": ("sbuf", [128, 1], "float32"),
+    "sqD": ("sbuf", [128, 1], "float32"),
+    "SI": ("sbuf", [128, 128], "float32"),
     "st": ("sbuf", [128, SW], "float32"),
     "G": ("sbuf", [128, 8, SW], "float32"),
     "rep": ("sbuf", [128, 7, 6], "float32"),
@@ -27,6 +29,8 @@ SCRATCH = {
     "W2": ("sbuf", [128, 4], "float32"),
     "w": ("sbuf", [128, 2], "float32"),
     "k": ("sbuf", [128, 2], "float32"),
+    "sz": ("sbuf", [128, 2], "float32"),
+    "rsw": ("sbuf", [128, 2], "float32"),
     "aon": ("sbuf", [128, 2], "float32"),
     "nega": ("sbuf", [128, 2], "float32"),
     "xc": ("sbuf", [128, 256], "float32"),
@@ -34,9 +38,7 @@ SCRATCH = {
     "prod": ("sbuf", [128, 256], "float32"),
     "u": ("sbuf", [128, 256], "float32"),
     "v": ("sbuf", [128, 256], "float32"),
-    "dz": ("sbuf", [128, 256], "float32"),
     "dw": ("sbuf", [128, 256], "float32"),
-    "sdB": ("sbuf", [128, 256], "float32"),
     "outb": ("sbuf", [128, 256], "float32"),
     "psx0": ("psum", [128, 512], "float32"),
     "psx1": ("psum", [128, 512], "float32"),
@@ -45,8 +47,9 @@ SCRATCH = {
     "y0": ("psum", [128, 512], "float32"),
     "y1": ("psum", [128, 512], "float32"),
     "y2": ("psum", [128, 512], "float32"),
+    "y3": ("psum", [128, 512], "float32"),
 }
-SEMAPHORES = (["ldx", "ldy", "ms", "first", "stat", "repd", "arr", "loc", "st0", "st1", "cp0", "cp1"]
+SEMAPHORES = (["ldx", "ldy", "ms", "mo", "md", "first", "stat", "repd", "arr", "loc", "st0", "st1", "cp0", "cp1"]
               + ["e%d" % i for i in range(NEV)])
 
 
@@ -84,8 +87,9 @@ def rank_program(g, core, T, topo):
     Q.dma_start(T.xF[:], T.x[:]).then_inc(sem.ldx, 16)
     A.dma_start(T.dyF[:], T.dy[:]).then_inc(sem.ldy, 16)
 
+    V.memset(T.Dc[:], float(D)).then_inc(sem.md, 1)
+    V.memset(T.ones[:], 1.0).then_inc(sem.mo, 1)
     fills = [
-        (T.ones[:], 1.0),
         (T.R[:, 0:1], -1.0), (T.R[:, 129:130], -1.0), (T.R[:, 130:131], -1.0 / 128.0),
         (T.G[:, 7, 0:6], 0.0), (T.G[:, 7, 6:8], D * EPS), (T.G[:, 7, 8:SW], 0.0),
         (T.st[:, 10:SW], 0.0),
@@ -93,12 +97,12 @@ def rank_program(g, core, T, topo):
     for ap, c in fills:
         V.memset(ap, c).then_inc(sem.ms, 1)
     M = len(fills)
-    e_id, e_di = ev(), ev()
-    g.wait_ge(sem.ms, M)
+    e_id, e_sq, e_si = ev(), ev(), ev()
+    A.wait_ge(sem.md, 1)
+    A.activation(T.sqD[:], T.Dc[:], F.Sqrt).then_inc(e_sq, 1)
+    g.wait_ge(sem.mo, 1)
     g.affine_select(T.R[:, 1:129], T.ones[:], [[-1, 128]], AluOpType.is_equal, 0.0, 0, 1).then_inc(e_id, 1)
     V.wait_ge(sem.ms, M)
-    V.wait_ge(e_id, 1)
-    V.tensor_scalar(T.DI[:], T.R[:, 1:129], float(D), None, mul).then_inc(e_di, 1)
 
     e_px, e_pd = [ev(), ev()], [ev(), ev()]
     e_xc, e_pr = [ev(), ev()], [ev(), ev()]
@@ -137,6 +141,7 @@ def rank_program(g, core, T, topo):
         ids.append(DstId(rid=rid, pnc=pid))
     g.wait_ge(sem.first, 2)
     g.remote_dma(T.G[:, rank, 0:4], T.st[:, 0:4], sem.arr, sem.loc, pid1, rid1, m1)
+    g.wait_ge(sem.ms, M)
     g.wait_ge(sem.stat, NSTAT)
     g.remote_dma_fused([RemoteDMATransfer(dst_ids=ids, dma_engine_mask=m5, remote_sem=sem.arr,
                                           srcs=[T.st[:]], dsts=[T.G[:, rank, :] for _ in rest], alu_op=0)],
@@ -158,6 +163,9 @@ def rank_program(g, core, T, topo):
     for r in range(NR):
         V.tensor_copy(T.rep[:, r, :], T.st[:, 0:6]).then_inc(sem.repd, 1)
     V.tensor_scalar(T.aon[:], T.st[:, 4:6], 1.0 / 128.0, None, mul).then_inc(e_aon, 1)
+    V.wait_ge(e_id, 1)
+    V.wait_ge(e_sq, 1)
+    V.tensor_scalar(T.SI[:], T.R[:, 1:129], T.sqD[:, 0:1], None, mul).then_inc(e_si, 1)
 
     V.wait_ge(e_own, 1)
     V.wait_ge(sem.repd, NR)
@@ -181,7 +189,20 @@ def rank_program(g, core, T, topo):
     V.wait_ge(e[7], 1)
     V.tensor_tensor(T.W2[:], T.W1[:], T.Z[:], add).then_inc(e[8], 1)
 
-    e_ng, e_dya = [ev(), ev()], [ev(), ev()]
+    e_w, e_k, e_sz = ev(), ev(), ev()
+    e_ng, e_dya, e_rs, e_dw = [ev(), ev()], [ev(), ev()], [ev(), ev()], [ev(), ev()]
+    e_u, e_v = [ev(), ev()], [ev(), ev()]
+    V.wait_ge(e[8], 1)
+    V.reciprocal(T.w[:], T.W2[:, 0:2]).then_inc(e_w, 1)
+    V.wait_ge(e_w, 1)
+    V.tensor_tensor(T.k[:], T.W2[:, 2:4], T.w[:], mul).then_inc(e_k, 1)
+    V.wait_ge(e_k, 1)
+    for h in range(2):
+        V.tensor_scalar(T.u[:, H[h]], T.xc[:, H[h]], T.Ph[:, 2 + h:3 + h], T.k[:, h:h + 1], sub, mul).then_inc(e_u[h], 1)
+        V.wait_ge(e_u[h], 1)
+        V.wait_ge(e_dya[h], 1)
+        V.tensor_tensor(T.v[:, H[h]], psd[h][:, 1:129], T.u[:, H[h]], sub).then_inc(e_v[h], 1)
+
     A.wait_ge(e[4], 1)
     A.wait_ge(e_aon, 1)
     A.wait_ge(sem.stat, NSTAT)
@@ -189,62 +210,30 @@ def rank_program(g, core, T, topo):
     for h in range(2):
         A.activation(T.nega[:, h:h + 1], T.S[:, 4 + h:5 + h], F.Identity, bias=T.aon[:, h:h + 1],
                      scale=1.0 / D).then_inc(e_ng[h], 1)
+    A.wait_ge(e[8], 1)
+    A.activation(T.sz[:], T.W2[:, 0:2], F.Sqrt).then_inc(e_sz, 1)
     for h in range(2):
         A.wait_ge(e_ng[h], 1)
         A.activation(psd[h][:, 1:129], psd[h][:, 1:129], F.Identity, bias=T.nega[:, h:h + 1]).then_inc(e_dya[h], 1)
+        if h == 0:
+            A.wait_ge(e_sz, 1)
+            A.wait_ge(e_w, 1)
+            A.wait_ge(e_si, 1)
+        A.activation(T.rsw[:, h:h + 1], T.sz[:, h:h + 1], F.Copy, scale=T.w[:, h:h + 1]).then_inc(e_rs[h], 1)
+        A.wait_ge(e_rs[h], 1)
+        A.activation(T.dw[:, H[h]], T.SI[:], F.Copy, scale=T.rsw[:, h:h + 1]).then_inc(e_dw[h], 1)
 
     half = [(c * CW) // 128 for c in range(NCH)]
-    low = [c * CW - 128 * half[c] for c in range(NCH)]
     col = [slice(c * CW, (c + 1) * CW) for c in range(NCH)]
-    bc = [T.psx0[:, 0:CW]] + [T.psx1[:, (c - 1) * CW:c * CW] for c in range(1, NCH)]
-    yt = [T.y0[:, 0:CW], T.y0[:, CW:2 * CW], T.y1[:, 0:CW], T.y2[:, 0:CW]]
-    e_dz, e_bc, e_dw, e_vt, e_s = ([ev() for _ in range(NCH)] for _ in range(5))
-
-    V.wait_ge(e[8], 1)
-    for c in range(NCH):
-        h = half[c]
-        V.tensor_scalar(T.dz[:, col[c]], T.R[:, 1 + low[c]:1 + low[c] + CW], T.W2[:, h:h + 1], None,
-                        mul).then_inc(e_dz[c], 1)
-    e_w, e_k = ev(), ev()
-    e_u, e_v = [ev(), ev()], [ev(), ev()]
-    V.reciprocal(T.w[:], T.W2[:, 0:2]).then_inc(e_w, 1)
-    V.wait_ge(e_w, 1)
-    V.tensor_tensor(T.k[:], T.W2[:, 2:4], T.w[:], mul).then_inc(e_k, 1)
-    V.wait_ge(e_k, 1)
-    V.wait_ge(e_di, 1)
-    for h in range(2):
-        V.tensor_scalar(T.u[:, H[h]], T.xc[:, H[h]], T.Ph[:, 2 + h:3 + h], T.k[:, h:h + 1], sub, mul).then_inc(e_u[h], 1)
-        V.wait_ge(e_u[h], 1)
-        V.wait_ge(e_dya[h], 1)
-        V.tensor_tensor(T.v[:, H[h]], psd[h][:, 1:129], T.u[:, H[h]], sub).then_inc(e_v[h], 1)
-        for c in range(NCH):
-            if half[c] == h:
-                V.tensor_scalar(T.dw[:, col[c]], T.DI[:, low[c]:low[c] + CW], T.w[:, h:h + 1], None,
-                                mul).then_inc(e_dw[c], 1)
-
-    for c in range(NCH):
-        P.wait_ge(e_dz[c], 1)
-        P.matmul(bc[c], T.ones[:], T.dz[:, col[c]], True, True).then_inc(e_bc[c], 1)
+    yt = [T.y0[:, 0:CW], T.y1[:, 0:CW], T.y2[:, 0:CW], T.y3[:, 0:CW]]
+    e_vt = [ev() for _ in range(NCH)]
+    cp = [sem.cp0, sem.cp1]
     for c in range(NCH):
         P.wait_ge(e_v[half[c]], 1)
-        P.wait_ge(e_dw[c], 1)
+        P.wait_ge(e_dw[half[c]], 1)
         P.matmul(yt[c], T.v[:, H[half[c]]], T.dw[:, col[c]], True, True).then_inc(e_vt[c], 1)
-
-    for c in range(NCH):
-        if c == 0:
-            A.wait_ge(e_bc[0], 1)
-        elif c == 1:
-            for j in range(1, NCH):
-                A.wait_ge(e_bc[j], 1)
-        A.activation(T.sdB[:, col[c]], bc[c], F.Sqrt, scale=1.0 / D).then_inc(e_s[c], 1)
-
-    cp = [sem.cp0, sem.cp1]
-    V.wait_ge(e_vt[0], 1)
-    V.wait_ge(e_vt[1], 1)
-    for c in range(NCH):
         V.wait_ge(e_vt[c], 1)
-        V.wait_ge(e_s[c], 1)
-        V.tensor_tensor(T.outb[:, col[c]], yt[c], T.sdB[:, col[c]], mul).then_inc(cp[half[c]], 1)
+        V.tensor_copy(T.outb[:, col[c]], yt[c]).then_inc(cp[half[c]], 1)
     Q.wait_ge(cp[0], NCH // 2)
     Q.dma_start(T.dx[:, H[0]], T.outb[:, H[0]]).then_inc(sem.st0, 16)
     A.wait_ge(cp[1], NCH // 2)

from concourse.bass import DstId, RemoteDMATransfer
from concourse.mybir import AluOpType, AxisListType, ActivationFunctionType

NR = 7
D = 128 * NR
EPS = 0.01
SW = 16
NEV = 64
NCH = 4
CW = 256 // NCH

SCRATCH = {
    "xF": ("sbuf", [128, 256], "float32"),
    "dyF": ("sbuf", [128, 256], "float32"),
    "ones": ("sbuf", [128, 128], "float32"),
    "R": ("sbuf", [128, 131], "float32"),
    "Dc": ("sbuf", [128, 1], "float32"),
    "sqD": ("sbuf", [128, 1], "float32"),
    "SI": ("sbuf", [128, 128], "float32"),
    "st": ("sbuf", [128, SW], "float32"),
    "G": ("sbuf", [128, 8, SW], "float32"),
    "rep": ("sbuf", [128, 7, 6], "float32"),
    "T1": ("sbuf", [128, 4, SW], "float32"),
    "T2": ("sbuf", [128, 2, SW], "float32"),
    "S": ("sbuf", [128, SW], "float32"),
    "Ph": ("sbuf", [128, 4], "float32"),
    "Z": ("sbuf", [128, 4], "float32"),
    "W1": ("sbuf", [128, 4], "float32"),
    "W2": ("sbuf", [128, 4], "float32"),
    "w": ("sbuf", [128, 2], "float32"),
    "k": ("sbuf", [128, 2], "float32"),
    "sz": ("sbuf", [128, 2], "float32"),
    "rsw": ("sbuf", [128, 2], "float32"),
    "aon": ("sbuf", [128, 2], "float32"),
    "nega": ("sbuf", [128, 2], "float32"),
    "xc": ("sbuf", [128, 256], "float32"),
    "junk": ("sbuf", [128, 256], "float32"),
    "prod": ("sbuf", [128, 256], "float32"),
    "u": ("sbuf", [128, 256], "float32"),
    "v": ("sbuf", [128, 256], "float32"),
    "dw": ("sbuf", [128, 256], "float32"),
    "outb": ("sbuf", [128, 256], "float32"),
    "psx0": ("psum", [128, 512], "float32"),
    "psx1": ("psum", [128, 512], "float32"),
    "psd0": ("psum", [128, 512], "float32"),
    "psd1": ("psum", [128, 512], "float32"),
    "y0": ("psum", [128, 512], "float32"),
    "y1": ("psum", [128, 512], "float32"),
    "y2": ("psum", [128, 512], "float32"),
    "y3": ("psum", [128, 512], "float32"),
}
SEMAPHORES = (["ldx", "ldy", "ms", "mo", "md", "first", "stat", "repd", "arr", "loc", "st0", "st1", "cp0", "cp1"]
              + ["e%d" % i for i in range(NEV)])


def _send_mask(topo, src, dsts):
    m = None
    for d in dsts:
        if not topo.may_write(src, d):
            raise ValueError("core %d may not write to core %d" % (src, d))
        m = topo.mask(src, d) if m is None else (m & topo.mask(src, d))
    return m, bin(m).count("1")


def _plan(cores, r):
    nxt = cores[(r + 1) % len(cores)]
    return nxt, [c for c in cores if c != cores[r] and c != nxt]


def rank_program(g, core, T, topo):
    rank = T.rank_of(core)
    if rank is None:
        return
    V, A, P, Q = g.vector, g.scalar, g.tensor, g.sync
    add, sub, mul = AluOpType.add, AluOpType.subtract, AluOpType.mult
    F = ActivationFunctionType
    sem = T.sem
    cnt = [0]

    def ev():
        cnt[0] += 1
        return sem["e%d" % (cnt[0] - 1)]

    H = [slice(0, 128), slice(128, 256)]
    psx, psd = [T.psx0, T.psx1], [T.psd0, T.psd1]

    Q.dma_start(T.xF[:], T.x[:]).then_inc(sem.ldx, 16)
    A.dma_start(T.dyF[:], T.dy[:]).then_inc(sem.ldy, 16)

    V.memset(T.Dc[:], float(D)).then_inc(sem.md, 1)
    V.memset(T.ones[:], 1.0).then_inc(sem.mo, 1)
    fills = [
        (T.R[:, 0:1], -1.0), (T.R[:, 129:130], -1.0), (T.R[:, 130:131], -1.0 / 128.0),
        (T.G[:, 7, 0:6], 0.0), (T.G[:, 7, 6:8], D * EPS), (T.G[:, 7, 8:SW], 0.0),
        (T.st[:, 10:SW], 0.0),
    ]
    for ap, c in fills:
        V.memset(ap, c).then_inc(sem.ms, 1)
    M = len(fills)
    e_id, e_sq, e_si = ev(), ev(), ev()
    A.wait_ge(sem.md, 1)
    A.activation(T.sqD[:], T.Dc[:], F.Sqrt).then_inc(e_sq, 1)
    g.wait_ge(sem.mo, 1)
    g.affine_select(T.R[:, 1:129], T.ones[:], [[-1, 128]], AluOpType.is_equal, 0.0, 0, 1).then_inc(e_id, 1)
    V.wait_ge(sem.ms, M)

    e_px, e_pd = [ev(), ev()], [ev(), ev()]
    e_xc, e_pr = [ev(), ev()], [ev(), ev()]
    P.wait_ge(sem.ms, M)
    P.wait_ge(e_id, 1)
    P.wait_ge(sem.ldx, 16)
    for h in range(2):
        P.matmul(psx[h][:, 0:130], T.xF[:, H[h]], T.R[:, 1:131], True, True).then_inc(e_px[h], 1)
        V.wait_ge(e_px[h], 1)
        V.tensor_copy(T.st[:, h:h + 3:2], psx[h][:, 128:130]).then_inc(sem.first, 1)
        V.tensor_scalar(T.xc[:, H[h]], psx[h][:, 0:128], psx[h][:, 129:130], None, add).then_inc(e_xc[h], 1)
        A.wait_ge(e_xc[h], 1)
        A.activation(T.junk[:, H[h]], T.xc[:, H[h]], F.Square, accum_out=T.st[:, 6 + h:7 + h]).then_inc(sem.stat, 1)
    P.wait_ge(sem.ldy, 16)
    for h in range(2):
        P.matmul(psd[h][:, 0:129], T.dyF[:, H[h]], T.R[:, 0:129], True, True).then_inc(e_pd[h], 1)
        V.wait_ge(e_pd[h], 1)
        V.wait_ge(e_xc[h], 1)
        V.tensor_tensor(T.prod[:, H[h]], psd[h][:, 1:129], T.xc[:, H[h]], mul).then_inc(e_pr[h], 1)
        if h == 0:
            V.tensor_copy(T.st[:, 4:5], psd[h][:, 0:1]).then_inc(sem.stat, 1)
        else:
            A.wait_ge(e_pr[h], 1)
            A.activation(T.st[:, 5:6], psd[h][:, 0:1], F.Copy).then_inc(sem.stat, 1)
        V.wait_ge(e_pr[h], 1)
        V.tensor_reduce(T.st[:, 8 + h:9 + h], T.prod[:, H[h]], AxisListType.X, add).then_inc(sem.stat, 1)
    NSTAT = 6

    nxt, rest = _plan(T.cores, rank)
    m1, b1 = _send_mask(topo, core, [nxt])
    m5, b5 = _send_mask(topo, core, rest)
    rid1, pid1, _se1 = topo.addr(nxt)
    ids = []
    for c in rest:
        rid, pid, _se = topo.addr(c)
        ids.append(DstId(rid=rid, pnc=pid))
    g.wait_ge(sem.first, 2)
    g.remote_dma(T.G[:, rank, 0:4], T.st[:, 0:4], sem.arr, sem.loc, pid1, rid1, m1)
    g.wait_ge(sem.ms, M)
    g.wait_ge(sem.stat, NSTAT)
    g.remote_dma_fused([RemoteDMATransfer(dst_ids=ids, dma_engine_mask=m5, remote_sem=sem.arr,
                                          srcs=[T.st[:]], dsts=[T.G[:, rank, :] for _ in rest], alu_op=0)],
                       local_sem=sem.loc)
    g.remote_dma(T.G[:, rank, 4:SW], T.st[:, 4:SW], sem.arr, sem.loc, pid1, rid1, m1)
    expected = 0
    for r in range(NR):
        if r != rank:
            n_r, rest_r = _plan(T.cores, r)
            if n_r == core:
                expected += 2 * _send_mask(topo, T.cores[r], [core])[1]
            else:
                expected += _send_mask(topo, T.cores[r], rest_r)[1]

    e_own, e_aon = ev(), ev()
    V.wait_ge(sem.first, 2)
    V.wait_ge(sem.stat, NSTAT)
    V.tensor_copy(T.G[:, rank, :], T.st[:]).then_inc(e_own, 1)
    for r in range(NR):
        V.tensor_copy(T.rep[:, r, :], T.st[:, 0:6]).then_inc(sem.repd, 1)
    V.tensor_scalar(T.aon[:], T.st[:, 4:6], 1.0 / 128.0, None, mul).then_inc(e_aon, 1)
    V.wait_ge(e_id, 1)
    V.wait_ge(e_sq, 1)
    V.tensor_scalar(T.SI[:], T.R[:, 1:129], T.sqD[:, 0:1], None, mul).then_inc(e_si, 1)

    V.wait_ge(e_own, 1)
    V.wait_ge(sem.repd, NR)
    V.wait_ge(sem.arr, expected)
    e = [ev() for _ in range(9)]
    V.tensor_tensor(T.G[:, 0:7, 0:6], T.G[:, 0:7, 0:6], T.rep[:], sub).then_inc(e[0], 1)
    V.wait_ge(e[0], 1)
    V.tensor_tensor(T.G[:, 0:7, 10:14], T.G[:, 0:7, 0:4], T.G[:, 0:7, 2:6], mul).then_inc(e[1], 1)
    V.wait_ge(e[1], 1)
    V.tensor_tensor(T.T1[:], T.G[:, 0:4, :], T.G[:, 4:8, :], add).then_inc(e[2], 1)
    V.wait_ge(e[2], 1)
    V.tensor_tensor(T.T2[:], T.T1[:, 0:2, :], T.T1[:, 2:4, :], add).then_inc(e[3], 1)
    V.wait_ge(e[3], 1)
    V.tensor_tensor(T.S[:], T.T2[:, 0, :], T.T2[:, 1, :], add).then_inc(e[4], 1)
    V.wait_ge(e[4], 1)
    V.tensor_scalar(T.Ph[:], T.S[:, 0:4], -1.0 / NR, None, mul).then_inc(e[5], 1)
    V.tensor_tensor(T.W1[:], T.S[:, 6:10], T.S[:, 10:14], add).then_inc(e[6], 1)
    V.wait_ge(e[5], 1)
    V.tensor_tensor(T.Z[:], T.Ph[:], T.S[:, 2:6], mul).then_inc(e[7], 1)
    V.wait_ge(e[6], 1)
    V.wait_ge(e[7], 1)
    V.tensor_tensor(T.W2[:], T.W1[:], T.Z[:], add).then_inc(e[8], 1)

    e_w, e_k, e_sz = ev(), ev(), ev()
    e_ng, e_dya, e_rs, e_dw = [ev(), ev()], [ev(), ev()], [ev(), ev()], [ev(), ev()]
    e_u, e_v = [ev(), ev()], [ev(), ev()]
    V.wait_ge(e[8], 1)
    V.reciprocal(T.w[:], T.W2[:, 0:2]).then_inc(e_w, 1)
    V.wait_ge(e_w, 1)
    V.tensor_tensor(T.k[:], T.W2[:, 2:4], T.w[:], mul).then_inc(e_k, 1)
    V.wait_ge(e_k, 1)
    for h in range(2):
        V.tensor_scalar(T.u[:, H[h]], T.xc[:, H[h]], T.Ph[:, 2 + h:3 + h], T.k[:, h:h + 1], sub, mul).then_inc(e_u[h], 1)
        V.wait_ge(e_u[h], 1)
        V.wait_ge(e_dya[h], 1)
        V.tensor_tensor(T.v[:, H[h]], psd[h][:, 1:129], T.u[:, H[h]], sub).then_inc(e_v[h], 1)

    A.wait_ge(e[4], 1)
    A.wait_ge(e_aon, 1)
    A.wait_ge(sem.stat, NSTAT)
    A.wait_ge(e_pr[0], 1)
    for h in range(2):
        A.activation(T.nega[:, h:h + 1], T.S[:, 4 + h:5 + h], F.Identity, bias=T.aon[:, h:h + 1],
                     scale=1.0 / D).then_inc(e_ng[h], 1)
    A.wait_ge(e[8], 1)
    A.activation(T.sz[:], T.W2[:, 0:2], F.Sqrt).then_inc(e_sz, 1)
    for h in range(2):
        A.wait_ge(e_ng[h], 1)
        A.activation(psd[h][:, 1:129], psd[h][:, 1:129], F.Identity, bias=T.nega[:, h:h + 1]).then_inc(e_dya[h], 1)
        if h == 0:
            A.wait_ge(e_sz, 1)
            A.wait_ge(e_w, 1)
            A.wait_ge(e_si, 1)
        A.activation(T.rsw[:, h:h + 1], T.sz[:, h:h + 1], F.Copy, scale=T.w[:, h:h + 1]).then_inc(e_rs[h], 1)
        A.wait_ge(e_rs[h], 1)
        A.activation(T.dw[:, H[h]], T.SI[:], F.Copy, scale=T.rsw[:, h:h + 1]).then_inc(e_dw[h], 1)

    half = [(c * CW) // 128 for c in range(NCH)]
    col = [slice(c * CW, (c + 1) * CW) for c in range(NCH)]
    yt = [T.y0[:, 0:CW], T.y1[:, 0:CW], T.y2[:, 0:CW], T.y3[:, 0:CW]]
    e_vt = [ev() for _ in range(NCH)]
    cp = [sem.cp0, sem.cp1]
    for c in range(NCH):
        P.wait_ge(e_v[half[c]], 1)
        P.wait_ge(e_dw[half[c]], 1)
        P.matmul(yt[c], T.v[:, H[half[c]]], T.dw[:, col[c]], True, True).then_inc(e_vt[c], 1)
        V.wait_ge(e_vt[c], 1)
        V.tensor_copy(T.outb[:, col[c]], yt[c]).then_inc(cp[half[c]], 1)
    Q.wait_ge(cp[0], NCH // 2)
    Q.dma_start(T.dx[:, H[0]], T.outb[:, H[0]]).then_inc(sem.st0, 16)
    A.wait_ge(cp[1], NCH // 2)
    A.dma_start(T.dx[:, H[1]], T.outb[:, H[1]]).then_inc(sem.st1, 16)

    g.wait_ge(sem.loc, 2 * b1 + b5)
    Q.wait_ge(sem.st0, 16)
    A.wait_ge(sem.st1, 16)
